import numpy as np
import ml_dtypes


def mxq(x, axis, fmt="e4m3"):
    dtype, down = {"e4m3": (ml_dtypes.float8_e4m3fn, 7), "e5m2": (ml_dtypes.float8_e5m2, 14)}[fmt]
    v = np.moveaxis(np.asarray(x, np.float32).astype(ml_dtypes.bfloat16).astype(np.float64), axis, -1)
    blocks = v.reshape(v.shape[:-1] + (-1, 32))
    amax = np.abs(blocks).max(-1, keepdims=True)
    byte = np.maximum(np.where(amax > 0, np.frexp(amax)[1] - 1 + 127, 0) - down, 1)
    scale = np.exp2(byte - 127.0)
    codes = (blocks / scale).astype(np.float32).astype(dtype).astype(np.float64)
    return np.moveaxis((codes * scale).reshape(v.shape), -1, axis)


WIDE = False


def mx_kscale(k):
    if not WIDE:
        return np.ones(k)
    levels = np.array([30, -30])
    if k % 512:
        return np.exp2(np.random.permutation(np.resize(levels, k // 32))).repeat(32)
    a = np.empty((k // 512, 16))
    for p in range(k // 512):
        a[p, :8] = np.random.permutation(np.resize(levels, 8))
        for g in range(8):
            far = levels[np.abs(levels - a[p, g]) >= 10]
            a[p, g + 8] = far[np.random.randint(len(far))]
    return np.exp2(a.ravel()).repeat(32)


def f64(x):
    return np.asarray(x).astype(np.float64)


def striped(idx):
    return np.tile(np.asarray(idx).reshape(-1, 16).T, (8, 1)).astype(np.uint16)


def unstriped(offs):
    return offs[:16].T.reshape(-1).astype(np.int64)


E2M1 = np.array([0.0, 0.5, 1.0, 1.5, 2.0, 3.0, 4.0, 6.0, -0.0, -0.5, -1.0, -1.5, -2.0, -3.0, -4.0, -6.0])


def pack_weight(w, fmt):
    k, n = w.shape
    w = f64(np.asarray(w, np.float32).astype(ml_dtypes.bfloat16)).reshape(k // 32, 32, n)
    amax = np.abs(w).max(1)
    if fmt in ("e4m3", "e5m2"):
        byte = np.frexp(amax)[1] - 1 + 127 - (7 if fmt == "e4m3" else 14)
    else:
        mant, ex = np.frexp(amax / 6.0)
        byte = np.where(mant > 0.5, ex, ex - 1) + 127
    byte = np.clip(np.where(amax > 0, byte, 1), 1, 254)
    scaled = (w * np.exp2(127.0 - byte)[:, None, :]).reshape(k, n).astype(np.float32)
    by_word = np.ascontiguousarray(scaled.reshape(k // 512, 128, 4, n).transpose(0, 1, 3, 2))
    if fmt in ("e4m3", "e5m2"):
        words = by_word.astype(ml_dtypes.float8_e4m3fn if fmt == "e4m3" else ml_dtypes.float8_e5m2).view(np.uint8)
    else:
        c = by_word.astype(ml_dtypes.float4_e2m1fn).view(np.uint8) & 0xF
        words = (c[..., 0::2] | (c[..., 1::2] << 4)).reshape(k // 512, 128, 2 * n)
    return np.ascontiguousarray(words), np.ascontiguousarray(byte.astype(np.uint8).reshape(k // 512, 16, n))


def unpack_weight(words, scales, fmt):
    g, _, n = scales.shape
    words = np.ascontiguousarray(words).reshape(g, 128, n, -1)
    if fmt in ("e4m3", "e5m2"):
        vals = words.view(ml_dtypes.float8_e4m3fn if fmt == "e4m3" else ml_dtypes.float8_e5m2).astype(np.float64)
    else:
        nib = np.empty((g, 128, n, 4), np.uint8)
        nib[..., 0::2] = words & 0xF
        nib[..., 1::2] = words >> 4
        vals = E2M1[nib]
    vals = vals * np.repeat(np.exp2(scales.astype(np.float64) - 127.0), 8, axis=1)[..., None]
    return vals.transpose(0, 1, 3, 2).reshape(g * 512, n)


K, T, J, I, R, V = 512, 512, 256, 256, 512, 512


def setup_inputs():
    n = np.random.standard_normal
    idx = np.random.permutation(T)[:J]
    idx2 = np.random.permutation(T)[:I]
    idx3 = np.random.permutation(V)[:I]
    fk = mx_kscale(K)
    fr = mx_kscale(R)
    xtp = pack_weight(n((K, T)) / fk[:, None], "e2m1")
    wap = pack_weight(n((K, R)) * 0.5 / np.sqrt(K) * fk[:, None] * fr, "e2m1")
    wbp = pack_weight(n((K, R)) * 1 / np.sqrt(K) * fk[:, None] / fr, "e5m2")
    return {
        "xt_words": xtp[0],
        "xt_scales": xtp[1],
        "wa_words": wap[0],
        "wa_scales": wap[1],
        "oa": (n((R, J)) * 0.5 * fr[:, None]).astype(np.float32),
        "wb_words": wbp[0],
        "wb_scales": wbp[1],
        "tb": (n((R, V)) * 0.5 / fr[:, None]).astype(np.float32),
        "offs": striped(idx),
        "offs2": striped(idx2),
        "offs3": striped(idx3),
    }


def reference(xt_words, xt_scales, wa_words, wa_scales, oa, wb_words, wb_scales, tb, offs, offs2, offs3):
    idx = unstriped(offs)
    idx2 = unstriped(offs2)
    idx3 = unstriped(offs3)
    xtu = unpack_weight(xt_words, xt_scales, "e2m1")
    wau = unpack_weight(wa_words, wa_scales, "e2m1")
    wbu = unpack_weight(wb_words, wb_scales, "e5m2")
    xtidxg = xtu[:, idx]
    za = wau.T @ xtidxg
    ha = np.maximum(za, f64(oa))
    xtidx2g = xtu[:, idx2]
    zb = wbu.T @ xtidx2g
    hb = np.maximum(zb - f64(tb)[:, idx3], 0.0)
    haq = mxq(ha, 0, "e5m2")
    hbq = mxq(hb, 0, "e4m3")
    a0 = haq.T @ hbq
    mn = np.mean(a0, axis=1, keepdims=True)
    y = 0.04 * np.maximum(a0 - mn, 0.0)
    return y

@@ -1,0 +1,182 @@
+from contextlib import ExitStack
+
+import concourse.mybir as mybir
+
+K, T, J, I, R, V = 512, 512, 256, 256, 512, 512
+FLOPS = 2 * K * R * J + 2 * K * R * I + 2 * R * J * I
+
+F32 = mybir.dt.float32
+BF16 = mybir.dt.bfloat16
+I32 = mybir.dt.int32
+U32 = mybir.dt.uint32
+U16 = mybir.dt.uint16
+U8 = mybir.dt.uint8
+E2M1 = mybir.dt.float4_e2m1fn_x4
+E5M2 = mybir.dt.float8_e5m2_x4
+E4M3 = mybir.dt.float8_e4m3fn_x4
+ALU = mybir.AluOpType
+ACT = mybir.ActivationFunctionType
+
+P = 128
+PACK = 4
+BLOCKS = 16
+RUN = 8
+HALF = 128
+GAIN = 0.04
+
+
+def load_scales(queue, plane, scales):
+    rows = scales[0].bitcast(I32)
+    for a in range(4):
+        queue.dma_start(
+            out=plane[32 * a : 32 * (a + 1), :].bitcast(I32),
+            in_=rows[4 * a : 4 * (a + 1), :].unsqueeze(0).broadcast_to([8, 4, rows.shape[1]]),
+        )
+
+
+def deal(nc, dealt, natural):
+    nc.scalar.copy(
+        out=dealt[:].bitcast(U32).rearrange("p (t g w) -> p t g w", t=PACK, g=BLOCKS),
+        in_=natural[:].bitcast(U32).rearrange("p (g t w) -> p t g w", t=PACK, g=BLOCKS),
+    )
+
+
+def slot_rows(matrix, t):
+    return matrix.rearrange("(g t q) c -> t g q c", t=PACK, q=RUN)[t]
+
+
+def tile_list_meet_added_overtable_abovemean_kernel(
+    tc, xt_words, xt_scales, wa_words, wa_scales, oa, wb_words, wb_scales, tb, offs, offs2, offs3, out
+):
+    nc = tc.nc
+    with ExitStack() as ctx:
+        sb = ctx.enter_context(tc.tile_pool(name="sb", bufs=1))
+        ps = ctx.enter_context(tc.psum_pool(name="ps", bufs=1))
+
+        def tile(name, shape, dtype):
+            return sb.tile(shape, dtype, name=name, align_bytes=64)
+
+        rows_list = tile("rows_list", [P, J // 16], U16)
+        cols_list = tile("cols_list", [P, I // 16], U16)
+        table_list = tile("table_list", [P, I // 16], U16)
+        xt_w = tile("xt_w", [P, T], U16)
+        xt_s = tile("xt_s", [P, T], U8)
+        wa_w = tile("wa_w", [P, 2 * R], U8)
+        wa_s = tile("wa_s", [P, R], U8)
+        wb_w = tile("wb_w", [P, 4 * R], U8)
+        wb_s = tile("wb_s", [P, R], U8)
+        tb_sb = [tile("tb_sb%d" % t, [P, V], F32) for t in range(PACK)]
+        oa_sb = tile("oa_sb", [P, PACK, J], F32)
+
+        nc.sync.dma_start(cols_list[:], offs2)
+        nc.sync.dma_start(out=xt_w[:].bitcast(I32), in_=xt_words[0].bitcast(I32))
+        load_scales(nc.sync, xt_s, xt_scales)
+        load_scales(nc.gpsimd, wa_s, wa_scales)
+        for t in range(2):
+            nc.sync.dma_start(out=tb_sb[t][:], in_=slot_rows(tb, t))
+        nc.sync.dma_start(table_list[:], offs3)
+        nc.sync.dma_start(rows_list[:], offs)
+        nc.sync.dma_start(out=wb_w[:].bitcast(I32), in_=wb_words[0].rearrange("p c t -> p (c t)").bitcast(I32))
+        load_scales(nc.sync, wb_s, wb_scales)
+        for t in range(2, PACK):
+            nc.sync.dma_start(out=tb_sb[t][:], in_=slot_rows(tb, t))
+        nc.sync.dma_start(out=wa_w[:].bitcast(I32), in_=wa_words[0].bitcast(I32))
+        for t in range(PACK):
+            nc.sync.dma_start(out=oa_sb[:, t, :], in_=slot_rows(oa, t))
+
+        xb_w = tile("xb_w", [P, I], U16)
+        xb_s = tile("xb_s", [P, I], U8)
+        xa_w = tile("xa_w", [P, J], U16)
+        xa_s = tile("xa_s", [P, J], U8)
+        nc.vector.tensor_copy(xb_w[:], xt_w[:].indirect(cols_list[:]))
+        nc.vector.tensor_copy(xb_s[:], xt_s[:].indirect(cols_list[:]))
+        nc.vector.tensor_copy(xa_w[:], xt_w[:].indirect(rows_list[:]))
+        nc.vector.tensor_copy(xa_s[:], xt_s[:].indirect(rows_list[:]))
+
+        wb_wd = tile("wb_wd", [P, 4 * R], U8)
+        wb_sd = tile("wb_sd", [P, R], U8)
+        wa_wd = tile("wa_wd", [P, 2 * R], U8)
+        wa_sd = tile("wa_sd", [P, R], U8)
+        picked = [tile("picked%d" % u, [P, 2, I], F32) for u in range(2)]
+        for t in range(PACK):
+            nc.scalar.activation(picked[t // 2][:, t % 2, :], tb_sb[t][:].indirect(table_list[:]), ACT.Copy)
+            if t == 1:
+                deal(nc, wb_wd, wb_w)
+                deal(nc, wb_sd, wb_s)
+
+        deal(nc, wa_wd, wa_w)
+        deal(nc, wa_sd, wa_s)
+
+        diff = tile("diff", [P, PACK, I], F32)
+        for u in range(2):
+            zb = ps.tile([P, 2, I], F32, name="zb%d" % u)
+            for e in range(2):
+                t = 2 * u + e
+                nc.tensor.matmul_mx(
+                    out=zb[:, e, :],
+                    lhsT=wb_wd[:, 4 * P * t : 4 * P * (t + 1)].bitcast(E5M2),
+                    lhsT_scale=wb_sd[:, P * t : P * (t + 1)],
+                    rhs=xb_w[:].bitcast(E2M1),
+                    rhs_scale=xb_s[:],
+                    start=True,
+                    stop=True,
+                )
+            nc.vector.tensor_tensor(out=diff[:, 2 * u : 2 * u + 2, :], in0=zb[:], in1=picked[u][:], op=ALU.subtract)
+
+        hb = tile("hb", [P, I, PACK], BF16)
+        for h in range(2):
+            cols = slice(HALF * h, HALF * (h + 1))
+            nc.scalar.activation(
+                hb[:, cols, :].rearrange("p (c i) t -> p c t i", i=4),
+                diff[:, :, cols].rearrange("p t (c i) -> p c t i", i=4),
+                ACT.Relu,
+            )
+
+        ha = [tile("ha%d" % h, [P, HALF, PACK], BF16) for h in range(2)]
+        for h in range(2):
+            cols = slice(HALF * h, HALF * (h + 1))
+            za = ps.tile([P, PACK, HALF], F32, name="za%d" % h)
+            for t in range(PACK):
+                nc.tensor.matmul_mx(
+                    out=za[:, t, :],
+                    lhsT=wa_wd[:, 2 * P * t : 2 * P * (t + 1)].bitcast(E2M1),
+                    lhsT_scale=wa_sd[:, P * t : P * (t + 1)],
+                    rhs=xa_w[:, cols].bitcast(E2M1),
+                    rhs_scale=xa_s[:, cols],
+                    start=True,
+                    stop=True,
+                )
+            nc.vector.tensor_tensor(
+                out=ha[h][:].rearrange("p (c i) t -> p c t i", i=4),
+                in0=za[:].rearrange("p t (c i) -> p c t i", i=4),
+                in1=oa_sb[:, :, cols].rearrange("p t (c i) -> p c t i", i=4),
+                op=ALU.max,
+            )
+
+        hb_w = tile("hb_w", [P, I], U32)
+        hb_s = tile("hb_s", [P, I], U8)
+        nc.vector.quantize_mx(out=hb_w[:].bitcast(E4M3), scales=hb_s[:], in_=hb[:].rearrange("p i t -> p (i t)"))
+
+        for h in range(2):
+            ha_w = tile("ha_w%d" % h, [P, HALF], U32)
+            ha_s = tile("ha_s%d" % h, [P, HALF], U8)
+            nc.vector.quantize_mx(out=ha_w[:].bitcast(E5M2), scales=ha_s[:], in_=ha[h][:].rearrange("p j t -> p (j t)"))
+            a0 = ps.tile([P, I], F32, name="a0_%d" % h)
+            nc.tensor.matmul_mx(
+                out=a0[:],
+                lhsT=ha_w[:].bitcast(E5M2),
+                lhsT_scale=ha_s[:],
+                rhs=hb_w[:].bitcast(E4M3),
+                rhs_scale=hb_s[:],
+                start=True,
+                stop=True,
+            )
+            share = tile("share%d" % h, [P, I], F32)
+            neg_mean = tile("neg_mean%d" % h, [P, 1], F32)
+            result = tile("result%d" % h, [P, I], F32)
+            if h == 0:
+                nc.scalar.activation(share[:], a0[:], ACT.Copy, scale=-GAIN / I, accum_out=neg_mean[:])
+            else:
+                nc.vector.tensor_scalar(share[:], a0[:], -GAIN / I, None, ALU.mult, ALU.add, accum_out=neg_mean[:])
+            nc.scalar.activation(result[:], share[:], ACT.Relu, bias=neg_mean[:], scale=-float(I))
+            nc.sync.dma_start(out=out[HALF * h : HALF * (h + 1), :], in_=result[:])

@@ -25,19 +25,10 @@ HALF = 128
 GAIN = 0.04
 
 
-def load_scales(queue, plane, scales):
-    rows = scales[0].bitcast(I32)
-    for a in range(4):
-        queue.dma_start(
-            out=plane[32 * a : 32 * (a + 1), :].bitcast(I32),
-            in_=rows[4 * a : 4 * (a + 1), :].unsqueeze(0).broadcast_to([8, 4, rows.shape[1]]),
-        )
-
-
-def deal(nc, dealt, natural):
-    nc.scalar.copy(
-        out=dealt[:].bitcast(U32).rearrange("p (t g w) -> p t g w", t=PACK, g=BLOCKS),
-        in_=natural[:].bitcast(U32).rearrange("p (g t w) -> p t g w", t=PACK, g=BLOCKS),
+def dealt_views(dealt, natural, groups):
+    return (
+        dealt.bitcast(U32).rearrange("p (t g e) -> p t g e", t=PACK, g=groups),
+        natural.bitcast(U32).rearrange("p (g t e) -> p t g e", t=PACK, g=groups),
     )
 
 
@@ -53,8 +44,8 @@ def tile_list_meet_added_overtable_abovemean_kernel(
         sb = ctx.enter_context(tc.tile_pool(name="sb", bufs=1))
         ps = ctx.enter_context(tc.psum_pool(name="ps", bufs=1))
 
-        def tile(name, shape, dtype):
-            return sb.tile(shape, dtype, name=name, align_bytes=64)
+        def tile(name, shape, dtype, tag=""):
+            return sb.tile(shape, dtype, name=name, tag=tag, align_bytes=64)
 
         rows_list = tile("rows_list", [P, J // 16], U16)
         cols_list = tile("cols_list", [P, I // 16], U16)
@@ -62,73 +53,77 @@ def tile_list_meet_added_overtable_abovemean_kernel(
         xt_w = tile("xt_w", [P, T], U16)
         xt_s = tile("xt_s", [P, T], U8)
         wa_w = tile("wa_w", [P, 2 * R], U8)
-        wa_s = tile("wa_s", [P, R], U8)
         wb_w = tile("wb_w", [P, 4 * R], U8)
-        wb_s = tile("wb_s", [P, R], U8)
+        w_s = tile("w_s", [P, 2 * R], U8)
         tb_sb = [tile("tb_sb%d" % t, [P, V], F32) for t in range(PACK)]
-        oa_sb = tile("oa_sb", [P, PACK, J], F32)
 
+        nc.gpsimd.memset(xt_s[:].bitcast(I32), 0)
+        nc.gpsimd.memset(w_s[:, 0:R].bitcast(I32), 0)
+        nc.vector.memset(w_s[:, R : 2 * R].bitcast(I32), 0)
         nc.sync.dma_start(cols_list[:], offs2)
-        nc.sync.dma_start(out=xt_w[:].bitcast(I32), in_=xt_words[0].bitcast(I32))
-        load_scales(nc.sync, xt_s, xt_scales)
-        load_scales(nc.gpsimd, wa_s, wa_scales)
-        for t in range(2):
-            nc.sync.dma_start(out=tb_sb[t][:], in_=slot_rows(tb, t))
-        nc.sync.dma_start(table_list[:], offs3)
+        nc.scalar.dma_start(out=wa_w[:].bitcast(I32), in_=wa_words[0].bitcast(I32))
         nc.sync.dma_start(rows_list[:], offs)
+        nc.scalar.dma_start(out=xt_s[0:16, :].bitcast(I32), in_=xt_scales[0].bitcast(I32))
+        nc.sync.dma_start(out=w_s[0:16, R : 2 * R].bitcast(I32), in_=wa_scales[0].bitcast(I32))
+        nc.scalar.dma_start(out=w_s[0:16, 0:R].bitcast(I32), in_=wb_scales[0].bitcast(I32))
+        nc.sync.dma_start(out=tb_sb[0][:], in_=slot_rows(tb, 0))
+        nc.scalar.dma_start(out=tb_sb[1][:], in_=slot_rows(tb, 1))
+        nc.sync.dma_start(out=xt_w[:].bitcast(I32), in_=xt_words[0].bitcast(I32))
+        nc.sync.dma_start(table_list[:], offs3)
         nc.sync.dma_start(out=wb_w[:].bitcast(I32), in_=wb_words[0].rearrange("p c t -> p (c t)").bitcast(I32))
-        load_scales(nc.sync, wb_s, wb_scales)
         for t in range(2, PACK):
             nc.sync.dma_start(out=tb_sb[t][:], in_=slot_rows(tb, t))
-        nc.sync.dma_start(out=wa_w[:].bitcast(I32), in_=wa_words[0].bitcast(I32))
-        for t in range(PACK):
-            nc.sync.dma_start(out=oa_sb[:, t, :], in_=slot_rows(oa, t))
-
-        xb_w = tile("xb_w", [P, I], U16)
-        xb_s = tile("xb_s", [P, I], U8)
-        xa_w = tile("xa_w", [P, J], U16)
-        xa_s = tile("xa_s", [P, J], U8)
-        nc.vector.tensor_copy(xb_w[:], xt_w[:].indirect(cols_list[:]))
-        nc.vector.tensor_copy(xb_s[:], xt_s[:].indirect(cols_list[:]))
-        nc.vector.tensor_copy(xa_w[:], xt_w[:].indirect(rows_list[:]))
-        nc.vector.tensor_copy(xa_s[:], xt_s[:].indirect(rows_list[:]))
 
         wb_wd = tile("wb_wd", [P, 4 * R], U8)
-        wb_sd = tile("wb_sd", [P, R], U8)
         wa_wd = tile("wa_wd", [P, 2 * R], U8)
-        wa_sd = tile("wa_sd", [P, R], U8)
-        picked = [tile("picked%d" % u, [P, 2, I], F32) for u in range(2)]
+        x_s = tile("x_s", [P, I + J], U8, tag="chain")
+        planes = tile("planes", [P, 2 * R + I + J], U8)
+        nc.scalar.copy(*dealt_views(wa_wd[:], wa_w[:], BLOCKS))
+        nc.scalar.copy(*dealt_views(planes[:, 0 : 2 * R], w_s[:], 2 * BLOCKS))
+        nc.vector.tensor_copy(x_s[:, 0:I], xt_s[:].indirect(cols_list[:]))
+        nc.vector.tensor_copy(x_s[:, I : I + J], xt_s[:].indirect(rows_list[:]))
+        nc.vector.tensor_copy(planes[:, 2 * R :].bitcast(I32), x_s[:].bitcast(I32))
+        for a, queue in ((1, nc.sync), (2, nc.scalar), (3, nc.sync)):
+            queue.dma_start(out=planes[32 * a : 32 * a + 4, :].bitcast(I32), in_=planes[4 * a : 4 * a + 4, :].bitcast(I32))
+        oa_sb = tile("oa_sb", [P, PACK, J], F32, tag="chain")
         for t in range(PACK):
-            nc.scalar.activation(picked[t // 2][:, t % 2, :], tb_sb[t][:].indirect(table_list[:]), ACT.Copy)
-            if t == 1:
-                deal(nc, wb_wd, wb_w)
-                deal(nc, wb_sd, wb_s)
+            nc.sync.dma_start(out=oa_sb[:, t, :], in_=slot_rows(oa, t))
+        xb_s = planes[:, 2 * R : 2 * R + I]
+        xa_s = planes[:, 2 * R + I :]
 
-        deal(nc, wa_wd, wa_w)
-        deal(nc, wa_sd, wa_s)
+        xb_w = tile("xb_w", [P, I], U16)
+        xa_w = tile("xa_w", [P, J], U16)
+        nc.vector.tensor_copy(xb_w[:], xt_w[:].indirect(cols_list[:]))
+        nc.vector.tensor_copy(xa_w[:], xt_w[:].indirect(rows_list[:]))
 
-        diff = tile("diff", [P, PACK, I], F32)
-        for u in range(2):
-            zb = ps.tile([P, 2, I], F32, name="zb%d" % u)
-            for e in range(2):
-                t = 2 * u + e
-                nc.tensor.matmul_mx(
-                    out=zb[:, e, :],
-                    lhsT=wb_wd[:, 4 * P * t : 4 * P * (t + 1)].bitcast(E5M2),
-                    lhsT_scale=wb_sd[:, P * t : P * (t + 1)],
-                    rhs=xb_w[:].bitcast(E2M1),
-                    rhs_scale=xb_s[:],
-                    start=True,
-                    stop=True,
-                )
-            nc.vector.tensor_tensor(out=diff[:, 2 * u : 2 * u + 2, :], in0=zb[:], in1=picked[u][:], op=ALU.subtract)
+        picked = tile("picked", [P, PACK, I], F32)
+        for t in range(PACK):
+            window = tb_sb[t][:].indirect(table_list[:])
+            if t < 2:
+                nc.scalar.activation(picked[:, t, :], window, ACT.Copy)
+            else:
+                nc.vector.tensor_copy(picked[:, t, :], window)
+        nc.scalar.copy(*dealt_views(wb_wd[:], wb_w[:], BLOCKS))
 
         hb = tile("hb", [P, I, PACK], BF16)
         for h in range(2):
             cols = slice(HALF * h, HALF * (h + 1))
+            zb = ps.tile([P, PACK, HALF], F32, name="zb%d" % h)
+            for t in range(PACK):
+                nc.tensor.matmul_mx(
+                    out=zb[:, t, :],
+                    lhsT=wb_wd[:, 4 * P * t : 4 * P * (t + 1)].bitcast(E5M2),
+                    lhsT_scale=planes[:, 2 * P * t : 2 * P * t + P],
+                    rhs=xb_w[:, cols].bitcast(E2M1),
+                    rhs_scale=xb_s[:, cols],
+                    start=True,
+                    stop=True,
+                )
+            diff = tile("diff%d" % h, [P, PACK, HALF], F32)
+            nc.vector.tensor_tensor(out=diff[:], in0=zb[:], in1=picked[:, :, cols], op=ALU.subtract)
             nc.scalar.activation(
                 hb[:, cols, :].rearrange("p (c i) t -> p c t i", i=4),
-                diff[:, :, cols].rearrange("p t (c i) -> p c t i", i=4),
+                diff[:].rearrange("p t (c i) -> p c t i", i=4),
                 ACT.Relu,
             )
 
@@ -140,7 +135,7 @@ def tile_list_meet_added_overtable_abovemean_kernel(
                 nc.tensor.matmul_mx(
                     out=za[:, t, :],
                     lhsT=wa_wd[:, 2 * P * t : 2 * P * (t + 1)].bitcast(E2M1),
-                    lhsT_scale=wa_sd[:, P * t : P * (t + 1)],
+                    lhsT_scale=planes[:, 2 * P * t + P : 2 * P * (t + 1)],
                     rhs=xa_w[:, cols].bitcast(E2M1),
                     rhs_scale=xa_s[:, cols],
                     start=True,
@@ -153,7 +148,7 @@ def tile_list_meet_added_overtable_abovemean_kernel(
                 op=ALU.max,
             )
 
-        hb_w = tile("hb_w", [P, I], U32)
+        hb_w = tile("hb_w", [P, I], U32, tag="chain")
         hb_s = tile("hb_s", [P, I], U8)
         nc.vector.quantize_mx(out=hb_w[:].bitcast(E4M3), scales=hb_s[:], in_=hb[:].rearrange("p i t -> p (i t)"))
 

@@ -54,8 +54,8 @@ def tile_list_meet_added_overtable_abovemean_kernel(
         xt_s = tile("xt_s", [P, T], U8)
         wa_w = tile("wa_w", [P, 2 * R], U8)
         wb_w = tile("wb_w", [P, 4 * R], U8)
-        w_s = tile("w_s", [P, 2 * R], U8)
-        tb_sb = [tile("tb_sb%d" % t, [P, V], F32) for t in range(PACK)]
+        w_s = tile("w_s", [P, 2 * R], U8, tag="late_table")
+        tb_sb = [tile("tb_sb%d" % t, [P, V], F32) for t in range(PACK - 1)]
 
         nc.gpsimd.memset(xt_s[:].bitcast(I32), 0)
         nc.gpsimd.memset(w_s[:, 0:R].bitcast(I32), 0)
@@ -69,22 +69,23 @@ def tile_list_meet_added_overtable_abovemean_kernel(
         nc.sync.dma_start(out=tb_sb[0][:], in_=slot_rows(tb, 0))
         nc.scalar.dma_start(out=tb_sb[1][:], in_=slot_rows(tb, 1))
         nc.sync.dma_start(out=xt_w[:].bitcast(I32), in_=xt_words[0].bitcast(I32))
-        nc.sync.dma_start(table_list[:], offs3)
         nc.sync.dma_start(out=wb_w[:].bitcast(I32), in_=wb_words[0].rearrange("p c t -> p (c t)").bitcast(I32))
-        for t in range(2, PACK):
-            nc.sync.dma_start(out=tb_sb[t][:], in_=slot_rows(tb, t))
+        nc.sync.dma_start(table_list[:], offs3)
+        nc.sync.dma_start(out=tb_sb[2][:], in_=slot_rows(tb, 2))
 
         wb_wd = tile("wb_wd", [P, 4 * R], U8)
         wa_wd = tile("wa_wd", [P, 2 * R], U8)
         x_s = tile("x_s", [P, I + J], U8, tag="chain")
         planes = tile("planes", [P, 2 * R + I + J], U8)
         nc.scalar.copy(*dealt_views(wa_wd[:], wa_w[:], BLOCKS))
-        nc.scalar.copy(*dealt_views(planes[:, 0 : 2 * R], w_s[:], 2 * BLOCKS))
         nc.vector.tensor_copy(x_s[:, 0:I], xt_s[:].indirect(cols_list[:]))
         nc.vector.tensor_copy(x_s[:, I : I + J], xt_s[:].indirect(rows_list[:]))
+        nc.vector.tensor_copy(*dealt_views(planes[:, 0 : 2 * R], w_s[:], 2 * BLOCKS))
         nc.vector.tensor_copy(planes[:, 2 * R :].bitcast(I32), x_s[:].bitcast(I32))
         for a, queue in ((1, nc.sync), (2, nc.scalar), (3, nc.sync)):
             queue.dma_start(out=planes[32 * a : 32 * a + 4, :].bitcast(I32), in_=planes[4 * a : 4 * a + 4, :].bitcast(I32))
+        tb_sb.append(tile("tb_sb3", [P, V], F32, tag="late_table"))
+        nc.sync.dma_start(out=tb_sb[3][:], in_=slot_rows(tb, 3))
         oa_sb = tile("oa_sb", [P, PACK, J], F32, tag="chain")
         for t in range(PACK):
             nc.sync.dma_start(out=oa_sb[:, t, :], in_=slot_rows(oa, t))
@@ -96,14 +97,13 @@ def tile_list_meet_added_overtable_abovemean_kernel(
         nc.vector.tensor_copy(xb_w[:], xt_w[:].indirect(cols_list[:]))
         nc.vector.tensor_copy(xa_w[:], xt_w[:].indirect(rows_list[:]))
 
-        picked = tile("picked", [P, PACK, I], F32)
-        for t in range(PACK):
-            window = tb_sb[t][:].indirect(table_list[:])
-            if t < 2:
-                nc.scalar.activation(picked[:, t, :], window, ACT.Copy)
-            else:
-                nc.vector.tensor_copy(picked[:, t, :], window)
         nc.scalar.copy(*dealt_views(wb_wd[:], wb_w[:], BLOCKS))
+        picked = tile("picked", [P, PACK, I], F32)
+        for t in range(2):
+            nc.scalar.activation(picked[:, t, :], tb_sb[t][:].indirect(table_list[:]), ACT.Copy)
+        nc.vector.tensor_copy(picked[:, 2, :], tb_sb[2][:].indirect(table_list[:]))
+        nc.vector.tensor_copy(picked[:, 3, 0:HALF], tb_sb[3][:].indirect(table_list[:, 0:8]))
+        nc.scalar.activation(picked[:, 3, HALF:I], tb_sb[3][:].indirect(table_list[:, 8:16]), ACT.Copy)
 
         hb = tile("hb", [P, I, PACK], BF16)
         for h in range(2):

from contextlib import ExitStack

import concourse.mybir as mybir

K, T, J, I, R, V = 512, 512, 256, 256, 512, 512
FLOPS = 2 * K * R * J + 2 * K * R * I + 2 * R * J * I

F32 = mybir.dt.float32
BF16 = mybir.dt.bfloat16
I32 = mybir.dt.int32
U32 = mybir.dt.uint32
U16 = mybir.dt.uint16
U8 = mybir.dt.uint8
E2M1 = mybir.dt.float4_e2m1fn_x4
E5M2 = mybir.dt.float8_e5m2_x4
E4M3 = mybir.dt.float8_e4m3fn_x4
ALU = mybir.AluOpType
ACT = mybir.ActivationFunctionType

P = 128
PACK = 4
BLOCKS = 16
RUN = 8
HALF = 128
GAIN = 0.04


def dealt_views(dealt, natural, groups):
    return (
        dealt.bitcast(U32).rearrange("p (t g e) -> p t g e", t=PACK, g=groups),
        natural.bitcast(U32).rearrange("p (g t e) -> p t g e", t=PACK, g=groups),
    )


def slot_rows(matrix, t):
    return matrix.rearrange("(g t q) c -> t g q c", t=PACK, q=RUN)[t]


def tile_list_meet_added_overtable_abovemean_kernel(
    tc, xt_words, xt_scales, wa_words, wa_scales, oa, wb_words, wb_scales, tb, offs, offs2, offs3, out
):
    nc = tc.nc
    with ExitStack() as ctx:
        sb = ctx.enter_context(tc.tile_pool(name="sb", bufs=1))
        ps = ctx.enter_context(tc.psum_pool(name="ps", bufs=1))

        def tile(name, shape, dtype, tag=""):
            return sb.tile(shape, dtype, name=name, tag=tag, align_bytes=64)

        rows_list = tile("rows_list", [P, J // 16], U16)
        cols_list = tile("cols_list", [P, I // 16], U16)
        table_list = tile("table_list", [P, I // 16], U16)
        xt_w = tile("xt_w", [P, T], U16)
        xt_s = tile("xt_s", [P, T], U8)
        wa_w = tile("wa_w", [P, 2 * R], U8)
        wb_w = tile("wb_w", [P, 4 * R], U8)
        w_s = tile("w_s", [P, 2 * R], U8, tag="late_table")
        tb_sb = [tile("tb_sb%d" % t, [P, V], F32) for t in range(PACK - 1)]

        nc.gpsimd.memset(xt_s[:].bitcast(I32), 0)
        nc.gpsimd.memset(w_s[:, 0:R].bitcast(I32), 0)
        nc.vector.memset(w_s[:, R : 2 * R].bitcast(I32), 0)
        nc.sync.dma_start(cols_list[:], offs2)
        nc.scalar.dma_start(out=wa_w[:].bitcast(I32), in_=wa_words[0].bitcast(I32))
        nc.sync.dma_start(rows_list[:], offs)
        nc.scalar.dma_start(out=xt_s[0:16, :].bitcast(I32), in_=xt_scales[0].bitcast(I32))
        nc.sync.dma_start(out=w_s[0:16, R : 2 * R].bitcast(I32), in_=wa_scales[0].bitcast(I32))
        nc.scalar.dma_start(out=w_s[0:16, 0:R].bitcast(I32), in_=wb_scales[0].bitcast(I32))
        nc.sync.dma_start(out=tb_sb[0][:], in_=slot_rows(tb, 0))
        nc.scalar.dma_start(out=tb_sb[1][:], in_=slot_rows(tb, 1))
        nc.sync.dma_start(out=xt_w[:].bitcast(I32), in_=xt_words[0].bitcast(I32))
        nc.sync.dma_start(out=wb_w[:].bitcast(I32), in_=wb_words[0].rearrange("p c t -> p (c t)").bitcast(I32))
        nc.sync.dma_start(table_list[:], offs3)
        nc.sync.dma_start(out=tb_sb[2][:], in_=slot_rows(tb, 2))

        wb_wd = tile("wb_wd", [P, 4 * R], U8)
        wa_wd = tile("wa_wd", [P, 2 * R], U8)
        x_s = tile("x_s", [P, I + J], U8, tag="chain")
        planes = tile("planes", [P, 2 * R + I + J], U8)
        nc.scalar.copy(*dealt_views(wa_wd[:], wa_w[:], BLOCKS))
        nc.vector.tensor_copy(x_s[:, 0:I], xt_s[:].indirect(cols_list[:]))
        nc.vector.tensor_copy(x_s[:, I : I + J], xt_s[:].indirect(rows_list[:]))
        nc.vector.tensor_copy(*dealt_views(planes[:, 0 : 2 * R], w_s[:], 2 * BLOCKS))
        nc.vector.tensor_copy(planes[:, 2 * R :].bitcast(I32), x_s[:].bitcast(I32))
        for a, queue in ((1, nc.sync), (2, nc.scalar), (3, nc.sync)):
            queue.dma_start(out=planes[32 * a : 32 * a + 4, :].bitcast(I32), in_=planes[4 * a : 4 * a + 4, :].bitcast(I32))
        tb_sb.append(tile("tb_sb3", [P, V], F32, tag="late_table"))
        nc.sync.dma_start(out=tb_sb[3][:], in_=slot_rows(tb, 3))
        oa_sb = tile("oa_sb", [P, PACK, J], F32, tag="chain")
        for t in range(PACK):
            nc.sync.dma_start(out=oa_sb[:, t, :], in_=slot_rows(oa, t))
        xb_s = planes[:, 2 * R : 2 * R + I]
        xa_s = planes[:, 2 * R + I :]

        xb_w = tile("xb_w", [P, I], U16)
        xa_w = tile("xa_w", [P, J], U16)
        nc.vector.tensor_copy(xb_w[:], xt_w[:].indirect(cols_list[:]))
        nc.vector.tensor_copy(xa_w[:], xt_w[:].indirect(rows_list[:]))

        nc.scalar.copy(*dealt_views(wb_wd[:], wb_w[:], BLOCKS))
        picked = tile("picked", [P, PACK, I], F32)
        for t in range(2):
            nc.scalar.activation(picked[:, t, :], tb_sb[t][:].indirect(table_list[:]), ACT.Copy)
        nc.vector.tensor_copy(picked[:, 2, :], tb_sb[2][:].indirect(table_list[:]))
        nc.vector.tensor_copy(picked[:, 3, 0:HALF], tb_sb[3][:].indirect(table_list[:, 0:8]))
        nc.scalar.activation(picked[:, 3, HALF:I], tb_sb[3][:].indirect(table_list[:, 8:16]), ACT.Copy)

        hb = tile("hb", [P, I, PACK], BF16)
        for h in range(2):
            cols = slice(HALF * h, HALF * (h + 1))
            zb = ps.tile([P, PACK, HALF], F32, name="zb%d" % h)
            for t in range(PACK):
                nc.tensor.matmul_mx(
                    out=zb[:, t, :],
                    lhsT=wb_wd[:, 4 * P * t : 4 * P * (t + 1)].bitcast(E5M2),
                    lhsT_scale=planes[:, 2 * P * t : 2 * P * t + P],
                    rhs=xb_w[:, cols].bitcast(E2M1),
                    rhs_scale=xb_s[:, cols],
                    start=True,
                    stop=True,
                )
            diff = tile("diff%d" % h, [P, PACK, HALF], F32)
            nc.vector.tensor_tensor(out=diff[:], in0=zb[:], in1=picked[:, :, cols], op=ALU.subtract)
            nc.scalar.activation(
                hb[:, cols, :].rearrange("p (c i) t -> p c t i", i=4),
                diff[:].rearrange("p t (c i) -> p c t i", i=4),
                ACT.Relu,
            )

        ha = [tile("ha%d" % h, [P, HALF, PACK], BF16) for h in range(2)]
        for h in range(2):
            cols = slice(HALF * h, HALF * (h + 1))
            za = ps.tile([P, PACK, HALF], F32, name="za%d" % h)
            for t in range(PACK):
                nc.tensor.matmul_mx(
                    out=za[:, t, :],
                    lhsT=wa_wd[:, 2 * P * t : 2 * P * (t + 1)].bitcast(E2M1),
                    lhsT_scale=planes[:, 2 * P * t + P : 2 * P * (t + 1)],
                    rhs=xa_w[:, cols].bitcast(E2M1),
                    rhs_scale=xa_s[:, cols],
                    start=True,
                    stop=True,
                )
            nc.vector.tensor_tensor(
                out=ha[h][:].rearrange("p (c i) t -> p c t i", i=4),
                in0=za[:].rearrange("p t (c i) -> p c t i", i=4),
                in1=oa_sb[:, :, cols].rearrange("p t (c i) -> p c t i", i=4),
                op=ALU.max,
            )

        hb_w = tile("hb_w", [P, I], U32, tag="chain")
        hb_s = tile("hb_s", [P, I], U8)
        nc.vector.quantize_mx(out=hb_w[:].bitcast(E4M3), scales=hb_s[:], in_=hb[:].rearrange("p i t -> p (i t)"))

        for h in range(2):
            ha_w = tile("ha_w%d" % h, [P, HALF], U32)
            ha_s = tile("ha_s%d" % h, [P, HALF], U8)
            nc.vector.quantize_mx(out=ha_w[:].bitcast(E5M2), scales=ha_s[:], in_=ha[h][:].rearrange("p j t -> p (j t)"))
            a0 = ps.tile([P, I], F32, name="a0_%d" % h)
            nc.tensor.matmul_mx(
                out=a0[:],
                lhsT=ha_w[:].bitcast(E5M2),
                lhsT_scale=ha_s[:],
                rhs=hb_w[:].bitcast(E4M3),
                rhs_scale=hb_s[:],
                start=True,
                stop=True,
            )
            share = tile("share%d" % h, [P, I], F32)
            neg_mean = tile("neg_mean%d" % h, [P, 1], F32)
            result = tile("result%d" % h, [P, I], F32)
            if h == 0:
                nc.scalar.activation(share[:], a0[:], ACT.Copy, scale=-GAIN / I, accum_out=neg_mean[:])
            else:
                nc.vector.tensor_scalar(share[:], a0[:], -GAIN / I, None, ALU.mult, ALU.add, accum_out=neg_mean[:])
            nc.scalar.activation(result[:], share[:], ACT.Relu, bias=neg_mean[:], scale=-float(I))
            nc.sync.dma_start(out=out[HALF * h : HALF * (h + 1), :], in_=result[:])
